import numpy as np
import ml_dtypes


def mxq(x, axis, fmt="e4m3"):
    dtype, down = {"e4m3": (ml_dtypes.float8_e4m3fn, 7), "e5m2": (ml_dtypes.float8_e5m2, 14)}[fmt]
    v = np.moveaxis(np.asarray(x, np.float32).astype(ml_dtypes.bfloat16).astype(np.float64), axis, -1)
    blocks = v.reshape(v.shape[:-1] + (-1, 32))
    amax = np.abs(blocks).max(-1, keepdims=True)
    byte = np.maximum(np.where(amax > 0, np.frexp(amax)[1] - 1 + 127, 0) - down, 1)
    scale = np.exp2(byte - 127.0)
    codes = (blocks / scale).astype(np.float32).astype(dtype).astype(np.float64)
    return np.moveaxis((codes * scale).reshape(v.shape), -1, axis)


WIDE = False


def mx_kscale(k):
    if not WIDE:
        return np.ones(k)
    levels = np.array([30, -30])
    if k % 512:
        return np.exp2(np.random.permutation(np.resize(levels, k // 32))).repeat(32)
    a = np.empty((k // 512, 16))
    for p in range(k // 512):
        a[p, :8] = np.random.permutation(np.resize(levels, 8))
        for g in range(8):
            far = levels[np.abs(levels - a[p, g]) >= 10]
            a[p, g + 8] = far[np.random.randint(len(far))]
    return np.exp2(a.ravel()).repeat(32)


def f64(x):
    return np.asarray(x).astype(np.float64)


E2M1 = np.array([0.0, 0.5, 1.0, 1.5, 2.0, 3.0, 4.0, 6.0, -0.0, -0.5, -1.0, -1.5, -2.0, -3.0, -4.0, -6.0])


def pack_weight(w, fmt):
    k, n = w.shape
    w = f64(np.asarray(w, np.float32).astype(ml_dtypes.bfloat16)).reshape(k // 32, 32, n)
    amax = np.abs(w).max(1)
    if fmt == "e4m3":
        byte = np.frexp(amax)[1] - 1 + 127 - 7
    else:
        mant, ex = np.frexp(amax / 6.0)
        byte = np.where(mant > 0.5, ex, ex - 1) + 127
    byte = np.clip(np.where(amax > 0, byte, 1), 1, 254)
    scaled = (w * np.exp2(127.0 - byte)[:, None, :]).reshape(k, n).astype(np.float32)
    by_word = np.ascontiguousarray(scaled.reshape(k // 512, 128, 4, n).transpose(0, 1, 3, 2))
    if fmt == "e4m3":
        words = by_word.astype(ml_dtypes.float8_e4m3fn).view(np.uint8)
    else:
        c = by_word.astype(ml_dtypes.float4_e2m1fn).view(np.uint8) & 0xF
        words = (c[..., 0::2] | (c[..., 1::2] << 4)).reshape(k // 512, 128, 2 * n)
    return np.ascontiguousarray(words), np.ascontiguousarray(byte.astype(np.uint8).reshape(k // 512, 16, n))


def unpack_weight(words, scales, fmt):
    g, _, n = scales.shape
    words = np.ascontiguousarray(words).reshape(g, 128, n, -1)
    if fmt == "e4m3":
        vals = words.view(ml_dtypes.float8_e4m3fn).astype(np.float64)
    else:
        nib = np.empty((g, 128, n, 4), np.uint8)
        nib[..., 0::2] = words & 0xF
        nib[..., 1::2] = words >> 4
        vals = E2M1[nib]
    vals = vals * np.repeat(np.exp2(scales.astype(np.float64) - 127.0), 8, axis=1)[..., None]
    return vals.transpose(0, 1, 3, 2).reshape(g * 512, n)


def silu(v):
    return v / (1.0 + np.exp(-v))


K, L, T, N = 1024, 1024, 512, 512


def setup_inputs():
    n = np.random.standard_normal
    fk = mx_kscale(K)
    fl = mx_kscale(L)
    wap = pack_weight(n((K, N)) * 1 / np.sqrt(K) * fk[:, None], "e2m1")
    xqp = pack_weight(n((L, T)) / fl[:, None], "e4m3")
    wqp = pack_weight(n((L, N)) * 1 / np.sqrt(L) * fl[:, None], "e2m1")
    return {
        "xf": (n((K, T)) / fk[:, None]).astype(np.float32),
        "wa_words": wap[0],
        "wa_scales": wap[1],
        "xq_words": xqp[0],
        "xq_scales": xqp[1],
        "wq_words": wqp[0],
        "wq_scales": wqp[1],
    }


def reference(xf, wa_words, wa_scales, xq_words, xq_scales, wq_words, wq_scales):
    wau = unpack_weight(wa_words, wa_scales, "e2m1")
    xqu = unpack_weight(xq_words, xq_scales, "e4m3")
    wqu = unpack_weight(wq_words, wq_scales, "e2m1")
    xp = np.pad(f64(xf), ((0, 0), (1, 0)))[:, :T]
    d = f64(xf) - xp
    dq = mxq(d, 0, "e5m2")
    z = wau.T @ dq + wqu.T @ xqu
    y = silu(0.6 * z)
    return y

@@ -1,0 +1,123 @@
+from contextlib import ExitStack
+
+import concourse.mybir as mybir
+
+K, T, N = 1024, 512, 512
+FLOPS = 2 * 2 * K * T * N
+
+F32 = mybir.dt.float32
+BF16 = mybir.dt.bfloat16
+I32 = mybir.dt.int32
+U32 = mybir.dt.uint32
+U8 = mybir.dt.uint8
+E4M3 = mybir.dt.float8_e4m3fn_x4
+E5M2 = mybir.dt.float8_e5m2_x4
+E2M1 = mybir.dt.float4_e2m1fn_x4
+
+P = 128
+PACK = 4
+K_PASS = P * PACK
+PASSES = K // K_PASS
+PAD = 8
+RUN = 4
+CHUNKS = [(0, 0, 128), (0, 128, 256), (0, 256, 512), (1, 0, 256), (1, 256, 512)]
+
+
+def tile_mix_change_and_state_kernel(tc, xf, wa_words, wa_scales, xq_words, xq_scales, wq_words, wq_scales, out):
+    nc = tc.nc
+    with ExitStack() as ctx:
+        keep = ctx.enter_context(tc.tile_pool(name="keep", bufs=1))
+        psum = ctx.enter_context(tc.psum_pool(name="psum", bufs=1))
+        ctx.enter_context(tc.manual_schedule())
+
+        x = [keep.tile([P, PACK, PAD + T], F32, name=f"x{z}", align_bytes=64) for z in range(PASSES)]
+        d = [keep.tile([P, T, PACK], BF16, name=f"d{z}", align_bytes=64) for z in range(PASSES)]
+        d_codes = [keep.tile([P, T], U32, name=f"d_codes{z}", align_bytes=64) for z in range(PASSES)]
+        d_plane = [keep.tile([P, T], U8, name=f"d_plane{z}", align_bytes=64) for z in range(PASSES)]
+        wa = keep.tile([P, PASSES, 2 * N], U8, align_bytes=64)
+        wq = keep.tile([P, PASSES, 2 * N], U8, align_bytes=64)
+        xq = keep.tile([P, PASSES, T], U32, align_bytes=64)
+        wa_plane = keep.tile([P, PASSES, N], U8, align_bytes=64)
+        wq_plane = keep.tile([P, PASSES, N], U8, align_bytes=64)
+        xq_plane = keep.tile([P, PASSES, T], U8, align_bytes=64)
+
+        for z in range(PASSES):
+            nc.gpsimd.memset(x[z][:, :, 0:PAD], 0.0)
+        for plane in (wa_plane, wq_plane, xq_plane):
+            nc.vector.memset(plane[:].bitcast(I32), 0)
+
+        def load_x(c):
+            z, t0, t1 = CHUNKS[c]
+            rows = xf[z * K_PASS : (z + 1) * K_PASS, t0:t1].rearrange("(p j) t -> p j t", j=PACK)
+            nc.sync.dma_start(out=x[z][:, :, PAD + t0 : PAD + t1], in_=rows)
+
+        scale_rows = [
+            (plane, src, r)
+            for plane, src in ((wa_plane, wa_scales), (wq_plane, wq_scales), (xq_plane, xq_scales))
+            for r in range(4)
+        ]
+
+        def load_scales(first, last):
+            for plane, src, r in scale_rows[first:last]:
+                nc.sync.dma_start(
+                    out=plane[r:P:32, :, :].bitcast(I32),
+                    in_=src.rearrange("z (q r) n -> r q z n", r=4)[r].bitcast(I32),
+                )
+
+        load_x(0)
+        load_x(1)
+        load_x(2)
+        load_scales(0, 5)
+        load_x(3)
+        nc.sync.dma_start(out=wa[:].bitcast(I32), in_=wa_words.rearrange("z p b -> p z b").bitcast(I32))
+        load_x(4)
+        load_scales(5, 10)
+        nc.sync.dma_start(out=wq[:].bitcast(I32), in_=wq_words.rearrange("z p b -> p z b").bitcast(I32))
+        nc.sync.dma_start(out=xq[:].bitcast(I32), in_=xq_words.rearrange("z p t r -> p z (t r)").bitcast(I32))
+        load_scales(10, 12)
+
+        def change(c):
+            z, t0, t1 = CHUNKS[c]
+            nc.vector.tensor_tensor(
+                out=d[z][:, t0:t1, :].rearrange("p (c i) j -> p c j i", i=RUN),
+                in0=x[z][:, :, PAD + t0 : PAD + t1].rearrange("p j (c i) -> p c j i", i=RUN),
+                in1=x[z][:, :, PAD + t0 - 1 : PAD + t1 - 1].rearrange("p j (c i) -> p c j i", i=RUN),
+                op=mybir.AluOpType.subtract,
+            )
+
+        def quantize(c):
+            z, t0, t1 = CHUNKS[c]
+            nc.vector.quantize_mx(
+                out=d_codes[z][:, t0:t1].bitcast(E5M2),
+                scales=d_plane[z][:, t0:t1],
+                in_=d[z][:, t0:t1, :].rearrange("p t j -> p (t j)"),
+            )
+
+        change(0)
+        for c in range(1, len(CHUNKS)):
+            change(c)
+            quantize(c - 1)
+        quantize(len(CHUNKS) - 1)
+
+        acc = [psum.tile([P, T], F32, name=f"acc{m}") for m in range(N // P)]
+
+        def multiply(m, w, w_plane, z, moving, moving_plane, start, stop):
+            nc.tensor.matmul_mx(
+                out=acc[m][:],
+                lhsT=w[:, z, 2 * P * m : 2 * P * (m + 1)].bitcast(E2M1),
+                lhsT_scale=w_plane[:, z, P * m : P * (m + 1)],
+                rhs=moving,
+                rhs_scale=moving_plane,
+                start=start,
+                stop=stop,
+            )
+
+        for z in range(PASSES):
+            for m in range(N // P):
+                multiply(m, wa, wa_plane, z, d_codes[z][:].bitcast(E5M2), d_plane[z][:], z == 0, False)
+        for m in range(N // P):
+            for z in range(PASSES):
+                multiply(m, wq, wq_plane, z, xq[:, z, :].bitcast(E4M3), xq_plane[:, z, :], False, z == PASSES - 1)
+            y = keep.tile([P, T], F32, name=f"y{m}")
+            nc.scalar.activation(out=y[:], in_=acc[m][:], func=mybir.ActivationFunctionType.Silu, scale=0.6)
+            nc.sync.dma_start(out=out[P * m : P * (m + 1), :], in_=y[:])

@@ -20,7 +20,7 @@ K_PASS = P * PACK
 PASSES = K // K_PASS
 PAD = 8
 RUN = 4
-CHUNKS = [(0, 0, 128), (0, 128, 256), (0, 256, 512), (1, 0, 256), (1, 256, 512)]
+CHUNKS = [(0, 0, 256), (0, 256, 512), (1, 0, 256), (1, 256, 512)]
 
 
 def tile_mix_change_and_state_kernel(tc, xf, wa_words, wa_scales, xq_words, xq_scales, wq_words, wq_scales, out):
@@ -36,14 +36,15 @@ def tile_mix_change_and_state_kernel(tc, xf, wa_words, wa_scales, xq_words, xq_s
         d_plane = [keep.tile([P, T], U8, name=f"d_plane{z}", align_bytes=64) for z in range(PASSES)]
         wa = keep.tile([P, PASSES, 2 * N], U8, align_bytes=64)
         wq = keep.tile([P, PASSES, 2 * N], U8, align_bytes=64)
-        xq = keep.tile([P, PASSES, T], U32, align_bytes=64)
+        xq = [keep.tile([P, T], U32, name=f"xq{z}", align_bytes=64) for z in range(PASSES)]
         wa_plane = keep.tile([P, PASSES, N], U8, align_bytes=64)
         wq_plane = keep.tile([P, PASSES, N], U8, align_bytes=64)
         xq_plane = keep.tile([P, PASSES, T], U8, align_bytes=64)
 
         for z in range(PASSES):
             nc.gpsimd.memset(x[z][:, :, 0:PAD], 0.0)
-        for plane in (wa_plane, wq_plane, xq_plane):
+        nc.gpsimd.memset(xq_plane[:].bitcast(I32), 0)
+        for plane in (wa_plane, wq_plane):
             nc.vector.memset(plane[:].bitcast(I32), 0)
 
         def load_x(c):
@@ -51,30 +52,30 @@ def tile_mix_change_and_state_kernel(tc, xf, wa_words, wa_scales, xq_words, xq_s
             rows = xf[z * K_PASS : (z + 1) * K_PASS, t0:t1].rearrange("(p j) t -> p j t", j=PACK)
             nc.sync.dma_start(out=x[z][:, :, PAD + t0 : PAD + t1], in_=rows)
 
-        scale_rows = [
-            (plane, src, r)
-            for plane, src in ((wa_plane, wa_scales), (wq_plane, wq_scales), (xq_plane, xq_scales))
-            for r in range(4)
-        ]
-
-        def load_scales(first, last):
-            for plane, src, r in scale_rows[first:last]:
-                nc.sync.dma_start(
+        def load_scales(queue, plane, src):
+            for r in range(4):
+                queue.dma_start(
                     out=plane[r:P:32, :, :].bitcast(I32),
                     in_=src.rearrange("z (q r) n -> r q z n", r=4)[r].bitcast(I32),
                 )
 
+        def load_weights(w, words):
+            nc.sync.dma_start(out=w[:].bitcast(I32), in_=words.rearrange("z p b -> p z b").bitcast(I32))
+
+        def load_state(z):
+            nc.sync.dma_start(out=xq[z][:].bitcast(I32), in_=xq_words[z].rearrange("p t r -> p (t r)").bitcast(I32))
+
+        load_scales(nc.gpsimd, xq_plane, xq_scales)
         load_x(0)
         load_x(1)
         load_x(2)
-        load_scales(0, 5)
+        load_weights(wa, wa_words)
+        load_scales(nc.sync, wa_plane, wa_scales)
         load_x(3)
-        nc.sync.dma_start(out=wa[:].bitcast(I32), in_=wa_words.rearrange("z p b -> p z b").bitcast(I32))
-        load_x(4)
-        load_scales(5, 10)
-        nc.sync.dma_start(out=wq[:].bitcast(I32), in_=wq_words.rearrange("z p b -> p z b").bitcast(I32))
-        nc.sync.dma_start(out=xq[:].bitcast(I32), in_=xq_words.rearrange("z p t r -> p z (t r)").bitcast(I32))
-        load_scales(10, 12)
+        load_weights(wq, wq_words)
+        load_scales(nc.sync, wq_plane, wq_scales)
+        load_state(0)
+        load_state(1)
 
         def change(c):
             z, t0, t1 = CHUNKS[c]
@@ -93,11 +94,11 @@ def tile_mix_change_and_state_kernel(tc, xf, wa_words, wa_scales, xq_words, xq_s
                 in_=d[z][:, t0:t1, :].rearrange("p t j -> p (t j)"),
             )
 
-        change(0)
-        for c in range(1, len(CHUNKS)):
-            change(c)
-            quantize(c - 1)
-        quantize(len(CHUNKS) - 1)
+        for z in range(PASSES):
+            change(2 * z)
+            change(2 * z + 1)
+            quantize(2 * z)
+            quantize(2 * z + 1)
 
         acc = [psum.tile([P, T], F32, name=f"acc{m}") for m in range(N // P)]
 
@@ -112,12 +113,21 @@ def tile_mix_change_and_state_kernel(tc, xf, wa_words, wa_scales, xq_words, xq_s
                 stop=stop,
             )
 
-        for z in range(PASSES):
-            for m in range(N // P):
-                multiply(m, wa, wa_plane, z, d_codes[z][:].bitcast(E5M2), d_plane[z][:], z == 0, False)
+        def change_pass(m, z, start, stop):
+            multiply(m, wa, wa_plane, z, d_codes[z][:].bitcast(E5M2), d_plane[z][:], start, stop)
+
+        def state_pass(m, z, start, stop):
+            multiply(m, wq, wq_plane, z, xq[z][:].bitcast(E4M3), xq_plane[:, z, :], start, stop)
+
         for m in range(N // P):
-            for z in range(PASSES):
-                multiply(m, wq, wq_plane, z, xq[:, z, :].bitcast(E4M3), xq_plane[:, z, :], False, z == PASSES - 1)
-            y = keep.tile([P, T], F32, name=f"y{m}")
-            nc.scalar.activation(out=y[:], in_=acc[m][:], func=mybir.ActivationFunctionType.Silu, scale=0.6)
-            nc.sync.dma_start(out=out[P * m : P * (m + 1), :], in_=y[:])
+            change_pass(m, 0, True, False)
+        for m in range(N // P):
+            state_pass(m, 0, False, False)
+        for m in range(N // P):
+            state_pass(m, 1, False, False)
+            change_pass(m, 1, False, True)
+            last = m == N // P - 1
+            for h, (t0, t1) in enumerate([(0, T // 2), (T // 2, T)] if last else [(0, T)]):
+                y = keep.tile([P, t1 - t0], F32, name=f"y{m}_{h}")
+                nc.scalar.activation(out=y[:], in_=acc[m][:, t0:t1], func=mybir.ActivationFunctionType.Silu, scale=0.6)
+                nc.sync.dma_start(out=out[P * m : P * (m + 1), t0:t1], in_=y[:])

@@ -36,16 +36,15 @@ def tile_mix_change_and_state_kernel(tc, xf, wa_words, wa_scales, xq_words, xq_s
         d_plane = [keep.tile([P, T], U8, name=f"d_plane{z}", align_bytes=64) for z in range(PASSES)]
         wa = keep.tile([P, PASSES, 2 * N], U8, align_bytes=64)
         wq = keep.tile([P, PASSES, 2 * N], U8, align_bytes=64)
-        xq = [keep.tile([P, T], U32, name=f"xq{z}", align_bytes=64) for z in range(PASSES)]
+        xq = keep.tile([P, PASSES, T], U32, align_bytes=64)
         wa_plane = keep.tile([P, PASSES, N], U8, align_bytes=64)
         wq_plane = keep.tile([P, PASSES, N], U8, align_bytes=64)
         xq_plane = keep.tile([P, PASSES, T], U8, align_bytes=64)
 
-        for z in range(PASSES):
-            nc.gpsimd.memset(x[z][:, :, 0:PAD], 0.0)
-        nc.gpsimd.memset(xq_plane[:].bitcast(I32), 0)
-        for plane in (wa_plane, wq_plane):
+        for plane in (wa_plane, wq_plane, xq_plane):
             nc.vector.memset(plane[:].bitcast(I32), 0)
+        for z in range(PASSES):
+            nc.vector.memset(x[z][:, :, 0:PAD], 0.0)
 
         def load_x(c):
             z, t0, t1 = CHUNKS[c]
@@ -62,20 +61,16 @@ def tile_mix_change_and_state_kernel(tc, xf, wa_words, wa_scales, xq_words, xq_s
         def load_weights(w, words):
             nc.sync.dma_start(out=w[:].bitcast(I32), in_=words.rearrange("z p b -> p z b").bitcast(I32))
 
-        def load_state(z):
-            nc.sync.dma_start(out=xq[z][:].bitcast(I32), in_=xq_words[z].rearrange("p t r -> p (t r)").bitcast(I32))
-
-        load_scales(nc.gpsimd, xq_plane, xq_scales)
         load_x(0)
         load_x(1)
+        load_scales(nc.sync, wa_plane, wa_scales)
         load_x(2)
         load_weights(wa, wa_words)
-        load_scales(nc.sync, wa_plane, wa_scales)
         load_x(3)
         load_weights(wq, wq_words)
         load_scales(nc.sync, wq_plane, wq_scales)
-        load_state(0)
-        load_state(1)
+        nc.sync.dma_start(out=xq[:].bitcast(I32), in_=xq_words.rearrange("z p t r -> p z (t r)").bitcast(I32))
+        load_scales(nc.sync, xq_plane, xq_scales)
 
         def change(c):
             z, t0, t1 = CHUNKS[c]
@@ -86,8 +81,7 @@ def tile_mix_change_and_state_kernel(tc, xf, wa_words, wa_scales, xq_words, xq_s
                 op=mybir.AluOpType.subtract,
             )
 
-        def quantize(c):
-            z, t0, t1 = CHUNKS[c]
+        def quantize(z, t0, t1):
             nc.vector.quantize_mx(
                 out=d_codes[z][:, t0:t1].bitcast(E5M2),
                 scales=d_plane[z][:, t0:t1],
@@ -97,8 +91,8 @@ def tile_mix_change_and_state_kernel(tc, xf, wa_words, wa_scales, xq_words, xq_s
         for z in range(PASSES):
             change(2 * z)
             change(2 * z + 1)
-            quantize(2 * z)
-            quantize(2 * z + 1)
+            quantize(*CHUNKS[2 * z])
+            quantize(*CHUNKS[2 * z + 1])
 
         acc = [psum.tile([P, T], F32, name=f"acc{m}") for m in range(N // P)]
 
@@ -117,17 +111,15 @@ def tile_mix_change_and_state_kernel(tc, xf, wa_words, wa_scales, xq_words, xq_s
             multiply(m, wa, wa_plane, z, d_codes[z][:].bitcast(E5M2), d_plane[z][:], start, stop)
 
         def state_pass(m, z, start, stop):
-            multiply(m, wq, wq_plane, z, xq[z][:].bitcast(E4M3), xq_plane[:, z, :], start, stop)
+            multiply(m, wq, wq_plane, z, xq[:, z, :].bitcast(E4M3), xq_plane[:, z, :], start, stop)
 
         for m in range(N // P):
             change_pass(m, 0, True, False)
         for m in range(N // P):
-            state_pass(m, 0, False, False)
+            change_pass(m, 1, False, False)
         for m in range(N // P):
-            state_pass(m, 1, False, False)
-            change_pass(m, 1, False, True)
-            last = m == N // P - 1
-            for h, (t0, t1) in enumerate([(0, T // 2), (T // 2, T)] if last else [(0, T)]):
-                y = keep.tile([P, t1 - t0], F32, name=f"y{m}_{h}")
-                nc.scalar.activation(out=y[:], in_=acc[m][:, t0:t1], func=mybir.ActivationFunctionType.Silu, scale=0.6)
-                nc.sync.dma_start(out=out[P * m : P * (m + 1), t0:t1], in_=y[:])
+            state_pass(m, 0, False, False)
+            state_pass(m, 1, False, True)
+            y = keep.tile([P, T], F32, name=f"y{m}")
+            nc.scalar.activation(out=y[:], in_=acc[m][:], func=mybir.ActivationFunctionType.Silu, scale=0.6)
+            nc.sync.dma_start(out=out[P * m : P * (m + 1), :], in_=y[:])

from contextlib import ExitStack

import concourse.mybir as mybir

K, T, N = 1024, 512, 512
FLOPS = 2 * 2 * K * T * N

F32 = mybir.dt.float32
BF16 = mybir.dt.bfloat16
I32 = mybir.dt.int32
U32 = mybir.dt.uint32
U8 = mybir.dt.uint8
E4M3 = mybir.dt.float8_e4m3fn_x4
E5M2 = mybir.dt.float8_e5m2_x4
E2M1 = mybir.dt.float4_e2m1fn_x4

P = 128
PACK = 4
K_PASS = P * PACK
PASSES = K // K_PASS
PAD = 8
RUN = 4
CHUNKS = [(0, 0, 256), (0, 256, 512), (1, 0, 256), (1, 256, 512)]


def tile_mix_change_and_state_kernel(tc, xf, wa_words, wa_scales, xq_words, xq_scales, wq_words, wq_scales, out):
    nc = tc.nc
    with ExitStack() as ctx:
        keep = ctx.enter_context(tc.tile_pool(name="keep", bufs=1))
        psum = ctx.enter_context(tc.psum_pool(name="psum", bufs=1))
        ctx.enter_context(tc.manual_schedule())

        x = [keep.tile([P, PACK, PAD + T], F32, name=f"x{z}", align_bytes=64) for z in range(PASSES)]
        d = [keep.tile([P, T, PACK], BF16, name=f"d{z}", align_bytes=64) for z in range(PASSES)]
        d_codes = [keep.tile([P, T], U32, name=f"d_codes{z}", align_bytes=64) for z in range(PASSES)]
        d_plane = [keep.tile([P, T], U8, name=f"d_plane{z}", align_bytes=64) for z in range(PASSES)]
        wa = keep.tile([P, PASSES, 2 * N], U8, align_bytes=64)
        wq = keep.tile([P, PASSES, 2 * N], U8, align_bytes=64)
        xq = keep.tile([P, PASSES, T], U32, align_bytes=64)
        wa_plane = keep.tile([P, PASSES, N], U8, align_bytes=64)
        wq_plane = keep.tile([P, PASSES, N], U8, align_bytes=64)
        xq_plane = keep.tile([P, PASSES, T], U8, align_bytes=64)

        for plane in (wa_plane, wq_plane, xq_plane):
            nc.vector.memset(plane[:].bitcast(I32), 0)
        for z in range(PASSES):
            nc.vector.memset(x[z][:, :, 0:PAD], 0.0)

        def load_x(c):
            z, t0, t1 = CHUNKS[c]
            rows = xf[z * K_PASS : (z + 1) * K_PASS, t0:t1].rearrange("(p j) t -> p j t", j=PACK)
            nc.sync.dma_start(out=x[z][:, :, PAD + t0 : PAD + t1], in_=rows)

        def load_scales(queue, plane, src):
            for r in range(4):
                queue.dma_start(
                    out=plane[r:P:32, :, :].bitcast(I32),
                    in_=src.rearrange("z (q r) n -> r q z n", r=4)[r].bitcast(I32),
                )

        def load_weights(w, words):
            nc.sync.dma_start(out=w[:].bitcast(I32), in_=words.rearrange("z p b -> p z b").bitcast(I32))

        load_x(0)
        load_x(1)
        load_scales(nc.sync, wa_plane, wa_scales)
        load_x(2)
        load_weights(wa, wa_words)
        load_x(3)
        load_weights(wq, wq_words)
        load_scales(nc.sync, wq_plane, wq_scales)
        nc.sync.dma_start(out=xq[:].bitcast(I32), in_=xq_words.rearrange("z p t r -> p z (t r)").bitcast(I32))
        load_scales(nc.sync, xq_plane, xq_scales)

        def change(c):
            z, t0, t1 = CHUNKS[c]
            nc.vector.tensor_tensor(
                out=d[z][:, t0:t1, :].rearrange("p (c i) j -> p c j i", i=RUN),
                in0=x[z][:, :, PAD + t0 : PAD + t1].rearrange("p j (c i) -> p c j i", i=RUN),
                in1=x[z][:, :, PAD + t0 - 1 : PAD + t1 - 1].rearrange("p j (c i) -> p c j i", i=RUN),
                op=mybir.AluOpType.subtract,
            )

        def quantize(z, t0, t1):
            nc.vector.quantize_mx(
                out=d_codes[z][:, t0:t1].bitcast(E5M2),
                scales=d_plane[z][:, t0:t1],
                in_=d[z][:, t0:t1, :].rearrange("p t j -> p (t j)"),
            )

        for z in range(PASSES):
            change(2 * z)
            change(2 * z + 1)
            quantize(*CHUNKS[2 * z])
            quantize(*CHUNKS[2 * z + 1])

        acc = [psum.tile([P, T], F32, name=f"acc{m}") for m in range(N // P)]

        def multiply(m, w, w_plane, z, moving, moving_plane, start, stop):
            nc.tensor.matmul_mx(
                out=acc[m][:],
                lhsT=w[:, z, 2 * P * m : 2 * P * (m + 1)].bitcast(E2M1),
                lhsT_scale=w_plane[:, z, P * m : P * (m + 1)],
                rhs=moving,
                rhs_scale=moving_plane,
                start=start,
                stop=stop,
            )

        def change_pass(m, z, start, stop):
            multiply(m, wa, wa_plane, z, d_codes[z][:].bitcast(E5M2), d_plane[z][:], start, stop)

        def state_pass(m, z, start, stop):
            multiply(m, wq, wq_plane, z, xq[:, z, :].bitcast(E4M3), xq_plane[:, z, :], start, stop)

        for m in range(N // P):
            change_pass(m, 0, True, False)
        for m in range(N // P):
            change_pass(m, 1, False, False)
        for m in range(N // P):
            state_pass(m, 0, False, False)
            state_pass(m, 1, False, True)
            y = keep.tile([P, T], F32, name=f"y{m}")
            nc.scalar.activation(out=y[:], in_=acc[m][:], func=mybir.ActivationFunctionType.Silu, scale=0.6)
            nc.sync.dma_start(out=out[P * m : P * (m + 1), :], in_=y[:])
